import numpy as np
import ml_dtypes


def mxq(x, axis, fmt="e4m3"):
    dtype, down = {"e4m3": (ml_dtypes.float8_e4m3fn, 7), "e5m2": (ml_dtypes.float8_e5m2, 14)}[fmt]
    v = np.moveaxis(np.asarray(x, np.float32).astype(ml_dtypes.bfloat16).astype(np.float64), axis, -1)
    blocks = v.reshape(v.shape[:-1] + (-1, 32))
    amax = np.abs(blocks).max(-1, keepdims=True)
    byte = np.maximum(np.where(amax > 0, np.frexp(amax)[1] - 1 + 127, 0) - down, 1)
    scale = np.exp2(byte - 127.0)
    codes = (blocks / scale).astype(np.float32).astype(dtype).astype(np.float64)
    return np.moveaxis((codes * scale).reshape(v.shape), -1, axis)


WIDE = False


def mx_kscale(k):
    if not WIDE:
        return np.ones(k)
    levels = np.array([30, -30])
    if k % 512:
        return np.exp2(np.random.permutation(np.resize(levels, k // 32))).repeat(32)
    a = np.empty((k // 512, 16))
    for p in range(k // 512):
        a[p, :8] = np.random.permutation(np.resize(levels, 8))
        for g in range(8):
            far = levels[np.abs(levels - a[p, g]) >= 10]
            a[p, g + 8] = far[np.random.randint(len(far))]
    return np.exp2(a.ravel()).repeat(32)


def f64(x):
    return np.asarray(x).astype(np.float64)


def striped(idx):
    return np.tile(np.asarray(idx).reshape(-1, 16).T, (8, 1)).astype(np.uint16)


def unstriped(offs):
    return offs[:16].T.reshape(-1).astype(np.int64)


E2M1 = np.array([0.0, 0.5, 1.0, 1.5, 2.0, 3.0, 4.0, 6.0, -0.0, -0.5, -1.0, -1.5, -2.0, -3.0, -4.0, -6.0])


def pack_weight(w, fmt):
    k, n = w.shape
    w = f64(np.asarray(w, np.float32).astype(ml_dtypes.bfloat16)).reshape(k // 32, 32, n)
    amax = np.abs(w).max(1)
    if fmt in ("e4m3", "e5m2"):
        byte = np.frexp(amax)[1] - 1 + 127 - (7 if fmt == "e4m3" else 14)
    else:
        mant, ex = np.frexp(amax / 6.0)
        byte = np.where(mant > 0.5, ex, ex - 1) + 127
    byte = np.clip(np.where(amax > 0, byte, 1), 1, 254)
    scaled = (w * np.exp2(127.0 - byte)[:, None, :]).reshape(k, n).astype(np.float32)
    by_word = np.ascontiguousarray(scaled.reshape(k // 512, 128, 4, n).transpose(0, 1, 3, 2))
    if fmt in ("e4m3", "e5m2"):
        words = by_word.astype(ml_dtypes.float8_e4m3fn if fmt == "e4m3" else ml_dtypes.float8_e5m2).view(np.uint8)
    else:
        c = by_word.astype(ml_dtypes.float4_e2m1fn).view(np.uint8) & 0xF
        words = (c[..., 0::2] | (c[..., 1::2] << 4)).reshape(k // 512, 128, 2 * n)
    return np.ascontiguousarray(words), np.ascontiguousarray(byte.astype(np.uint8).reshape(k // 512, 16, n))


def unpack_weight(words, scales, fmt):
    g, _, n = scales.shape
    words = np.ascontiguousarray(words).reshape(g, 128, n, -1)
    if fmt in ("e4m3", "e5m2"):
        vals = words.view(ml_dtypes.float8_e4m3fn if fmt == "e4m3" else ml_dtypes.float8_e5m2).astype(np.float64)
    else:
        nib = np.empty((g, 128, n, 4), np.uint8)
        nib[..., 0::2] = words & 0xF
        nib[..., 1::2] = words >> 4
        vals = E2M1[nib]
    vals = vals * np.repeat(np.exp2(scales.astype(np.float64) - 127.0), 8, axis=1)[..., None]
    return vals.transpose(0, 1, 3, 2).reshape(g * 512, n)


K, T, Z, J, R, C, N, E = 512, 1024, 1024, 256, 512, 512, 256, 1024


def setup_inputs():
    n = np.random.standard_normal
    idx = np.random.permutation(T)[:J]
    idx2 = np.random.permutation(Z)[:J]
    idx3 = np.random.permutation(C)[:J]
    idx4 = np.random.permutation(C)[:J]
    idx5 = np.random.permutation(E)[:J]
    fk = mx_kscale(K)
    fr = mx_kscale(R)
    xtp = pack_weight(n((K, T)) / fk[:, None], "e5m2")
    xop = pack_weight(n((K, Z)) / fk[:, None], "e4m3")
    wp = pack_weight(n((K, R)) * 1 / np.sqrt(K) * fk[:, None] * fr, "e2m1")
    wbp = pack_weight(n((R, N)) * 1 / np.sqrt(R) / fr[:, None], "e2m1")
    return {
        "xt_words": xtp[0],
        "xt_scales": xtp[1],
        "xo_words": xop[0],
        "xo_scales": xop[1],
        "w_words": wp[0],
        "w_scales": wp[1],
        "wb_words": wbp[0],
        "wb_scales": wbp[1],
        "offs": striped(idx),
        "offs2": striped(idx2),
        "offs3": striped(idx3),
        "offs4": striped(idx4),
        "offs5": striped(idx5),
    }


def reference(xt_words, xt_scales, xo_words, xo_scales, w_words, w_scales, wb_words, wb_scales, offs, offs2, offs3, offs4, offs5):
    idx = unstriped(offs)
    idx2 = unstriped(offs2)
    idx3 = unstriped(offs3)
    idx4 = unstriped(offs4)
    idx5 = unstriped(offs5)
    xtu = unpack_weight(xt_words, xt_scales, "e5m2")
    xou = unpack_weight(xo_words, xo_scales, "e4m3")
    wu = unpack_weight(w_words, w_scales, "e2m1")
    wbu = unpack_weight(wb_words, wb_scales, "e2m1")
    xtidxg = xtu[:, idx]
    a = wu.T @ xtidxg
    xoidx2g = xou[:, idx2]
    b = wu.T @ xoidx2g
    pw = np.zeros((R, C))
    pw[:, idx3] = a
    hid = np.abs(pw[:, idx4] - b)
    hidq = mxq(hid, 0, "e4m3")
    p = wbu.T @ hidq
    y = np.zeros((N, E))
    y[:, idx5] = p
    return y

@@ -1,0 +1,171 @@
+from contextlib import ExitStack
+
+import concourse.mybir as mybir
+
+K, T, J, R, C, N, E = 512, 1024, 256, 512, 512, 256, 1024
+FLOPS = 2 * K * R * J * 2 + 2 * R * N * J
+
+F32 = mybir.dt.float32
+BF16 = mybir.dt.bfloat16
+I32 = mybir.dt.int32
+U32 = mybir.dt.uint32
+U16 = mybir.dt.uint16
+U8 = mybir.dt.uint8
+E4M3 = mybir.dt.float8_e4m3fn_x4
+E5M2 = mybir.dt.float8_e5m2_x4
+E2M1 = mybir.dt.float4_e2m1fn_x4
+COPY = mybir.ActivationFunctionType.Copy
+ABS = mybir.ActivationFunctionType.Abs
+SUB = mybir.AluOpType.subtract
+
+P = 128
+PACK = 4
+HALVES = 2
+JH = J // HALVES
+LC = J // 16
+LH = JH // 16
+
+
+def load_scale_rows(queue, plane, scales):
+    for q in range(4):
+        queue.dma_start(out=plane[32 * q : 32 * q + 4, :].bitcast(I32), in_=scales[0, 4 * q : 4 * q + 4, :].bitcast(I32))
+
+
+def move(nc, on_scalar, out, in_):
+    if on_scalar:
+        nc.scalar.activation(out=out, in_=in_, func=COPY)
+    else:
+        nc.vector.tensor_copy(out=out, in_=in_)
+
+
+def tile_list_oneforboth_board_one_scattered_kernel(
+    tc, xt_words, xt_scales, xo_words, xo_scales, w_words, w_scales, wb_words, wb_scales, offs, offs2, offs3, offs4, offs5, out
+):
+    nc = tc.nc
+    with ExitStack() as ctx:
+        lists = ctx.enter_context(tc.tile_pool(name="lists", bufs=1))
+        keep = ctx.enter_context(tc.tile_pool(name="keep", bufs=1))
+        psum = ctx.enter_context(tc.psum_pool(name="psum", bufs=1))
+
+        token_list = lists.tile([P, LC], U16, name="token_list")
+        note_list = lists.tile([P, LC], U16, name="note_list")
+        put_list = lists.tile([P, LC], U16, name="put_list")
+        read_list = lists.tile([P, LC], U16, name="read_list")
+        page_list = lists.tile([P, LC], U16, name="page_list")
+
+        xt_w = keep.tile([P, T], U32, name="xt_w", align_bytes=64)
+        xt_s = keep.tile([P, T], U8, name="xt_s", align_bytes=64)
+        xo_s = keep.tile([P, T], U8, name="xo_s", tag="page0", align_bytes=64)
+        w_raw = keep.tile([P, 2 * R], U8, name="w_raw", tag="words", align_bytes=64)
+        ws_raw = keep.tile([P, R], U8, name="ws_raw", tag="page1", align_bytes=64)
+        wb_w = keep.tile([P, 2 * N], U8, name="wb_w", align_bytes=64)
+        wb_s = keep.tile([P, N], U8, name="wb_s", align_bytes=64)
+        board = [keep.tile([P, C], F32, name="board%d" % t, align_bytes=64) for t in range(PACK)]
+
+        for plane in (xt_s, ws_raw, xo_s):
+            nc.vector.memset(plane[:].bitcast(I32), 0)
+        nc.gpsimd.memset(wb_s[:].bitcast(I32), 0)
+        for t in range(PACK):
+            nc.vector.memset(board[t][:], 0.0)
+
+        nc.sync.dma_start(token_list[:], offs)
+        nc.sync.dma_start(out=xt_w[:].bitcast(I32), in_=xt_words[0].rearrange("p c t -> p (c t)").bitcast(I32))
+        load_scale_rows(nc.scalar, xt_s, xt_scales)
+        nc.sync.dma_start(out=w_raw[:].bitcast(I32), in_=w_words[0].bitcast(I32))
+        load_scale_rows(nc.sync, ws_raw, w_scales)
+        nc.sync.dma_start(put_list[:], offs3)
+        nc.sync.dma_start(note_list[:], offs2)
+        nc.sync.dma_start(read_list[:], offs4)
+        nc.sync.dma_start(page_list[:], offs5)
+        load_scale_rows(nc.sync, xo_s, xo_scales)
+        nc.gpsimd.dma_start(out=wb_w[:].bitcast(I32), in_=wb_words[0].bitcast(I32))
+        load_scale_rows(nc.gpsimd, wb_s, wb_scales)
+
+        xtg_w = keep.tile([P, J], U32, name="xtg_w", align_bytes=64)
+        xtg_s = keep.tile([P, J], U8, name="xtg_s", align_bytes=64)
+        xog_w = keep.tile([P, J], U32, name="xog_w", align_bytes=64)
+        xog_s = keep.tile([P, J], U8, name="xog_s", align_bytes=64)
+        w_w = keep.tile([P, 2 * R], U8, name="w_w", align_bytes=64)
+        w_s = keep.tile([P, R], U8, name="w_s", align_bytes=64)
+
+        nc.vector.tensor_copy(out=xtg_s[:], in_=xt_s[:].indirect(token_list[:]))
+        nc.vector.tensor_copy(
+            out=w_w[:].bitcast(U16).rearrange("p (t m) -> p t m", t=PACK),
+            in_=w_raw[:].bitcast(U16).rearrange("p (m t) -> p t m", t=PACK),
+        )
+        xo_w = keep.tile([P, T], U32, name="xo_w", tag="words", align_bytes=64)
+        nc.sync.dma_start(out=xo_w[:].bitcast(I32), in_=xo_words[0].rearrange("p c t -> p (c t)").bitcast(I32))
+        nc.vector.tensor_copy(out=xtg_w[:], in_=xt_w[:].indirect(token_list[:]))
+        nc.vector.tensor_copy(
+            out=w_s[:].rearrange("p (t m) -> p t m", t=PACK),
+            in_=ws_raw[:].rearrange("p (m t) -> p t m", t=PACK),
+        )
+
+        def first_product(acc, t, codes, scales):
+            nc.tensor.matmul_mx(
+                out=acc,
+                lhsT=w_w[:, 2 * P * t : 2 * P * (t + 1)].bitcast(E2M1),
+                lhsT_scale=w_s[:, P * t : P * (t + 1)],
+                rhs=codes,
+                rhs_scale=scales,
+                start=True,
+                stop=True,
+            )
+
+        a_ps = [psum.tile([P, J], F32, name="a_ps%d" % t, tag="bank%d" % t) for t in range(PACK)]
+        for t in (0, 2, 1, 3):
+            first_product(a_ps[t][:], t, xtg_w[:].bitcast(E5M2), xtg_s[:])
+
+        nc.vector.tensor_copy(out=xog_w[:], in_=xo_w[:].indirect(note_list[:]))
+        nc.vector.tensor_copy(out=xog_s[:], in_=xo_s[:].indirect(note_list[:]))
+        page = [keep.tile([P, E], F32, name="page%d" % g, tag="page%d" % g, align_bytes=64) for g in range(2)]
+        for g in (1, 0):
+            nc.gpsimd.memset(page[g][:], 0.0)
+        b_ps = [psum.tile([P, PACK, JH], F32, name="b_ps%d" % h) for h in range(HALVES)]
+        for h in range(HALVES):
+            cols = slice(JH * h, JH * (h + 1))
+            for t in range(PACK):
+                first_product(b_ps[h][:, t, :], t, xog_w[:, cols].bitcast(E4M3), xog_s[:, cols])
+
+        a_sb = [keep.tile([P, J], F32, name="a_sb%d" % t) for t in range(PACK - 1)]
+        a_sb.append(keep.tile([P, J], F32, name="a_sb3", tag="words", align_bytes=64))
+        for t in range(PACK):
+            move(nc, t % 2 == 0, a_sb[t][:], a_ps[t][:])
+        for t in range(PACK):
+            move(nc, t % 2 == 0, board[t][:].indirect(put_list[:]), a_sb[t][:])
+
+        picked = [keep.tile([P, PACK, JH], F32, name="picked%d" % h) for h in range(HALVES)]
+        diff = [keep.tile([P, PACK, JH], F32, name="diff%d" % h) for h in range(HALVES)]
+        hid = [keep.tile([P, JH, PACK], BF16, name="hid%d" % h, align_bytes=64) for h in range(HALVES)]
+        hid_w = [keep.tile([P, JH], U32, name="hid_w%d" % h, align_bytes=64) for h in range(HALVES)]
+        hid_s = [keep.tile([P, JH], U8, name="hid_s%d" % h, align_bytes=64) for h in range(HALVES)]
+        for h in range(HALVES):
+            for t in range(PACK):
+                move(nc, t < PACK - 1, picked[h][:, t, :], board[t][:].indirect(read_list[:, LH * h : LH * (h + 1)]))
+        for h in range(HALVES):
+            nc.vector.tensor_tensor(out=diff[h][:], in0=picked[h][:], in1=b_ps[h][:], op=SUB)
+        for h in range(HALVES):
+            nc.scalar.activation(out=hid[h][:], in_=diff[h][:].rearrange("p t j -> p j t"), func=ABS)
+        for h in range(HALVES):
+            nc.vector.quantize_mx(out=hid_w[h][:].bitcast(E4M3), scales=hid_s[h][:], in_=hid[h][:].rearrange("p j t -> p (j t)"))
+
+        p_ps = {}
+        for h in range(HALVES):
+            for g in range(2):
+                p_ps[h, g] = psum.tile([P, JH], F32, name="p_ps%d%d" % (h, g), tag="bank%d" % (2 * h + g))
+                nc.tensor.matmul_mx(
+                    out=p_ps[h, g][:],
+                    lhsT=wb_w[:, 2 * P * g : 2 * P * (g + 1)].bitcast(E2M1),
+                    lhsT_scale=wb_s[:, P * g : P * (g + 1)],
+                    rhs=hid_w[h][:].bitcast(E4M3),
+                    rhs_scale=hid_s[h][:],
+                    start=True,
+                    stop=True,
+                )
+        for h in range(HALVES):
+            for g in range(2):
+                p_sb = keep.tile([P, JH], F32, name="p_sb%d%d" % (h, g))
+                move(nc, g == 0, p_sb[:], p_ps[h, g][:])
+                move(nc, g == 0, page[g][:].indirect(page_list[:, LH * h : LH * (h + 1)]), p_sb[:])
+        nc.scalar.dma_start(out=out[0:P, :], in_=page[0][:])
+        nc.sync.dma_start(out=out[P : 2 * P, :], in_=page[1][:])

@@ -26,9 +26,9 @@ LC = J // 16
 LH = JH // 16
 
 
-def load_scale_rows(queue, plane, scales):
+def load_scale_rows(queues, plane, scales):
     for q in range(4):
-        queue.dma_start(out=plane[32 * q : 32 * q + 4, :].bitcast(I32), in_=scales[0, 4 * q : 4 * q + 4, :].bitcast(I32))
+        queues[q].dma_start(out=plane[32 * q : 32 * q + 4, :].bitcast(I32), in_=scales[0, 4 * q : 4 * q + 4, :].bitcast(I32))
 
 
 def move(nc, on_scalar, out, in_):
@@ -56,7 +56,8 @@ def tile_list_oneforboth_board_one_scattered_kernel(
         xt_w = keep.tile([P, T], U32, name="xt_w", align_bytes=64)
         xt_s = keep.tile([P, T], U8, name="xt_s", align_bytes=64)
         xo_s = keep.tile([P, T], U8, name="xo_s", tag="page0", align_bytes=64)
-        w_raw = keep.tile([P, 2 * R], U8, name="w_raw", tag="words", align_bytes=64)
+        xo_w = keep.tile([P, T], U32, name="xo_w", tag="words", align_bytes=64)
+        w_raw = keep.tile([P, 2 * R], U8, name="w_raw", align_bytes=64)
         ws_raw = keep.tile([P, R], U8, name="ws_raw", tag="page1", align_bytes=64)
         wb_w = keep.tile([P, 2 * N], U8, name="wb_w", align_bytes=64)
         wb_s = keep.tile([P, N], U8, name="wb_s", align_bytes=64)
@@ -64,22 +65,24 @@ def tile_list_oneforboth_board_one_scattered_kernel(
 
         for plane in (xt_s, ws_raw, xo_s):
             nc.vector.memset(plane[:].bitcast(I32), 0)
-        nc.gpsimd.memset(wb_s[:].bitcast(I32), 0)
         for t in range(PACK):
             nc.vector.memset(board[t][:], 0.0)
+        nc.vector.memset(wb_s[:].bitcast(I32), 0)
 
+        on_sync = [nc.sync] * 4
+        nc.gpsimd.dma_start(out=xo_w[:].bitcast(I32), in_=xo_words[0].rearrange("p c t -> p (c t)").bitcast(I32))
         nc.sync.dma_start(token_list[:], offs)
         nc.sync.dma_start(out=xt_w[:].bitcast(I32), in_=xt_words[0].rearrange("p c t -> p (c t)").bitcast(I32))
-        load_scale_rows(nc.scalar, xt_s, xt_scales)
+        load_scale_rows(on_sync, xt_s, xt_scales)
         nc.sync.dma_start(out=w_raw[:].bitcast(I32), in_=w_words[0].bitcast(I32))
-        load_scale_rows(nc.sync, ws_raw, w_scales)
-        nc.sync.dma_start(put_list[:], offs3)
+        load_scale_rows(on_sync, ws_raw, w_scales)
         nc.sync.dma_start(note_list[:], offs2)
+        nc.sync.dma_start(put_list[:], offs3)
+        load_scale_rows([nc.sync] * 3 + [nc.gpsimd], xo_s, xo_scales)
         nc.sync.dma_start(read_list[:], offs4)
+        nc.sync.dma_start(out=wb_w[:].bitcast(I32), in_=wb_words[0].bitcast(I32))
+        load_scale_rows(on_sync, wb_s, wb_scales)
         nc.sync.dma_start(page_list[:], offs5)
-        load_scale_rows(nc.sync, xo_s, xo_scales)
-        nc.gpsimd.dma_start(out=wb_w[:].bitcast(I32), in_=wb_words[0].bitcast(I32))
-        load_scale_rows(nc.gpsimd, wb_s, wb_scales)
 
         xtg_w = keep.tile([P, J], U32, name="xtg_w", align_bytes=64)
         xtg_s = keep.tile([P, J], U8, name="xtg_s", align_bytes=64)
@@ -93,13 +96,9 @@ def tile_list_oneforboth_board_one_scattered_kernel(
             out=w_w[:].bitcast(U16).rearrange("p (t m) -> p t m", t=PACK),
             in_=w_raw[:].bitcast(U16).rearrange("p (m t) -> p t m", t=PACK),
         )
-        xo_w = keep.tile([P, T], U32, name="xo_w", tag="words", align_bytes=64)
-        nc.sync.dma_start(out=xo_w[:].bitcast(I32), in_=xo_words[0].rearrange("p c t -> p (c t)").bitcast(I32))
         nc.vector.tensor_copy(out=xtg_w[:], in_=xt_w[:].indirect(token_list[:]))
-        nc.vector.tensor_copy(
-            out=w_s[:].rearrange("p (t m) -> p t m", t=PACK),
-            in_=ws_raw[:].rearrange("p (m t) -> p t m", t=PACK),
-        )
+        for t in (0, 2, 1, 3):
+            nc.vector.tensor_copy(out=w_s[:, P * t : P * (t + 1)], in_=ws_raw[:, t : R : PACK])
 
         def first_product(acc, t, codes, scales):
             nc.tensor.matmul_mx(

@@ -56,7 +56,7 @@ def tile_list_oneforboth_board_one_scattered_kernel(
         xt_w = keep.tile([P, T], U32, name="xt_w", align_bytes=64)
         xt_s = keep.tile([P, T], U8, name="xt_s", align_bytes=64)
         xo_s = keep.tile([P, T], U8, name="xo_s", tag="page0", align_bytes=64)
-        xo_w = keep.tile([P, T], U32, name="xo_w", tag="words", align_bytes=64)
+        xo_w = keep.tile([P, T], U32, name="xo_w", align_bytes=64)
         w_raw = keep.tile([P, 2 * R], U8, name="w_raw", align_bytes=64)
         ws_raw = keep.tile([P, R], U8, name="ws_raw", tag="page1", align_bytes=64)
         wb_w = keep.tile([P, 2 * N], U8, name="wb_w", align_bytes=64)
@@ -65,20 +65,20 @@ def tile_list_oneforboth_board_one_scattered_kernel(
 
         for plane in (xt_s, ws_raw, xo_s):
             nc.vector.memset(plane[:].bitcast(I32), 0)
-        for t in range(PACK):
+        for t in (0, 1, 2, 3):
             nc.vector.memset(board[t][:], 0.0)
         nc.vector.memset(wb_s[:].bitcast(I32), 0)
 
         on_sync = [nc.sync] * 4
-        nc.gpsimd.dma_start(out=xo_w[:].bitcast(I32), in_=xo_words[0].rearrange("p c t -> p (c t)").bitcast(I32))
         nc.sync.dma_start(token_list[:], offs)
-        nc.sync.dma_start(out=xt_w[:].bitcast(I32), in_=xt_words[0].rearrange("p c t -> p (c t)").bitcast(I32))
         load_scale_rows(on_sync, xt_s, xt_scales)
-        nc.sync.dma_start(out=w_raw[:].bitcast(I32), in_=w_words[0].bitcast(I32))
-        load_scale_rows(on_sync, ws_raw, w_scales)
         nc.sync.dma_start(note_list[:], offs2)
+        nc.sync.dma_start(out=w_raw[:].bitcast(I32), in_=w_words[0].bitcast(I32))
+        nc.sync.dma_start(out=xt_w[:].bitcast(I32), in_=xt_words[0].rearrange("p c t -> p (c t)").bitcast(I32))
+        load_scale_rows(on_sync, ws_raw, w_scales)
+        nc.sync.dma_start(out=xo_w[:].bitcast(I32), in_=xo_words[0].rearrange("p c t -> p (c t)").bitcast(I32))
+        load_scale_rows(on_sync, xo_s, xo_scales)
         nc.sync.dma_start(put_list[:], offs3)
-        load_scale_rows([nc.sync] * 3 + [nc.gpsimd], xo_s, xo_scales)
         nc.sync.dma_start(read_list[:], offs4)
         nc.sync.dma_start(out=wb_w[:].bitcast(I32), in_=wb_words[0].bitcast(I32))
         load_scale_rows(on_sync, wb_s, wb_scales)
@@ -97,7 +97,7 @@ def tile_list_oneforboth_board_one_scattered_kernel(
             in_=w_raw[:].bitcast(U16).rearrange("p (m t) -> p t m", t=PACK),
         )
         nc.vector.tensor_copy(out=xtg_w[:], in_=xt_w[:].indirect(token_list[:]))
-        for t in (0, 2, 1, 3):
+        for t in (0, 1, 2, 3):
             nc.vector.tensor_copy(out=w_s[:, P * t : P * (t + 1)], in_=ws_raw[:, t : R : PACK])
 
         def first_product(acc, t, codes, scales):
@@ -111,27 +111,29 @@ def tile_list_oneforboth_board_one_scattered_kernel(
                 stop=True,
             )
 
-        a_ps = [psum.tile([P, J], F32, name="a_ps%d" % t, tag="bank%d" % t) for t in range(PACK)]
-        for t in (0, 2, 1, 3):
-            first_product(a_ps[t][:], t, xtg_w[:].bitcast(E5M2), xtg_s[:])
+        a_ps = [psum.tile([P, J], F32, name="a_ps%d" % t, tag="bank%d" % t) for t in range(2)]
+        a_ps23 = psum.tile([P, 2, J], F32, name="a_ps23", tag="bank2")
+        for t in range(PACK):
+            first_product(a_ps[t][:] if t < 2 else a_ps23[:, t - 2, :], t, xtg_w[:].bitcast(E5M2), xtg_s[:])
 
         nc.vector.tensor_copy(out=xog_w[:], in_=xo_w[:].indirect(note_list[:]))
         nc.vector.tensor_copy(out=xog_s[:], in_=xo_s[:].indirect(note_list[:]))
-        page = [keep.tile([P, E], F32, name="page%d" % g, tag="page%d" % g, align_bytes=64) for g in range(2)]
-        for g in (1, 0):
-            nc.gpsimd.memset(page[g][:], 0.0)
         b_ps = [psum.tile([P, PACK, JH], F32, name="b_ps%d" % h) for h in range(HALVES)]
         for h in range(HALVES):
             cols = slice(JH * h, JH * (h + 1))
             for t in range(PACK):
                 first_product(b_ps[h][:, t, :], t, xog_w[:, cols].bitcast(E4M3), xog_s[:, cols])
 
-        a_sb = [keep.tile([P, J], F32, name="a_sb%d" % t) for t in range(PACK - 1)]
-        a_sb.append(keep.tile([P, J], F32, name="a_sb3", tag="words", align_bytes=64))
+        a_sb = [keep.tile([P, J], F32, name="a_sb%d" % t) for t in range(2)]
+        a_sb23 = keep.tile([P, 2, J], F32, name="a_sb23", tag="page0", align_bytes=64)
+        for t in range(2):
+            move(nc, True, a_sb[t][:], a_ps[t][:])
+        move(nc, False, a_sb23[:], a_ps23[:])
         for t in range(PACK):
-            move(nc, t % 2 == 0, a_sb[t][:], a_ps[t][:])
-        for t in range(PACK):
-            move(nc, t % 2 == 0, board[t][:].indirect(put_list[:]), a_sb[t][:])
+            move(nc, t < 2, board[t][:].indirect(put_list[:]), a_sb[t][:] if t < 2 else a_sb23[:, t - 2, :])
+        page = [keep.tile([P, E], F32, name="page%d" % g, tag="page%d" % g, align_bytes=64) for g in range(2)]
+        for g in (1, 0):
+            nc.gpsimd.memset(page[g][:], 0.0)
 
         picked = [keep.tile([P, PACK, JH], F32, name="picked%d" % h) for h in range(HALVES)]
         diff = [keep.tile([P, PACK, JH], F32, name="diff%d" % h) for h in range(HALVES)]
@@ -140,31 +142,41 @@ def tile_list_oneforboth_board_one_scattered_kernel(
         hid_s = [keep.tile([P, JH], U8, name="hid_s%d" % h, align_bytes=64) for h in range(HALVES)]
         for h in range(HALVES):
             for t in range(PACK):
-                move(nc, t < PACK - 1, picked[h][:, t, :], board[t][:].indirect(read_list[:, LH * h : LH * (h + 1)]))
+                move(nc, (h, t) != (0, 3), picked[h][:, t, :], board[t][:].indirect(read_list[:, LH * h : LH * (h + 1)]))
         for h in range(HALVES):
             nc.vector.tensor_tensor(out=diff[h][:], in0=picked[h][:], in1=b_ps[h][:], op=SUB)
         for h in range(HALVES):
-            nc.scalar.activation(out=hid[h][:], in_=diff[h][:].rearrange("p t j -> p j t"), func=ABS)
+            nc.scalar.activation(
+                out=hid[h][:].rearrange("p (c i) t -> p c t i", i=4),
+                in_=diff[h][:].rearrange("p t (c i) -> p c t i", i=4),
+                func=ABS,
+            )
         for h in range(HALVES):
             nc.vector.quantize_mx(out=hid_w[h][:].bitcast(E4M3), scales=hid_s[h][:], in_=hid[h][:].rearrange("p j t -> p (j t)"))
 
-        p_ps = {}
-        for h in range(HALVES):
-            for g in range(2):
-                p_ps[h, g] = psum.tile([P, JH], F32, name="p_ps%d%d" % (h, g), tag="bank%d" % (2 * h + g))
-                nc.tensor.matmul_mx(
-                    out=p_ps[h, g][:],
-                    lhsT=wb_w[:, 2 * P * g : 2 * P * (g + 1)].bitcast(E2M1),
-                    lhsT_scale=wb_s[:, P * g : P * (g + 1)],
-                    rhs=hid_w[h][:].bitcast(E4M3),
-                    rhs_scale=hid_s[h][:],
-                    start=True,
-                    stop=True,
-                )
-        for h in range(HALVES):
-            for g in range(2):
-                p_sb = keep.tile([P, JH], F32, name="p_sb%d%d" % (h, g))
-                move(nc, g == 0, p_sb[:], p_ps[h, g][:])
-                move(nc, g == 0, page[g][:].indirect(page_list[:, LH * h : LH * (h + 1)]), p_sb[:])
+        def second_product(acc, h, g):
+            nc.tensor.matmul_mx(
+                out=acc,
+                lhsT=wb_w[:, 2 * P * g : 2 * P * (g + 1)].bitcast(E2M1),
+                lhsT_scale=wb_s[:, P * g : P * (g + 1)],
+                rhs=hid_w[h][:].bitcast(E4M3),
+                rhs_scale=hid_s[h][:],
+                start=True,
+                stop=True,
+            )
+
+        first_ps = psum.tile([P, 2, JH], F32, name="first_ps", tag="bank0")
+        last_ps = [psum.tile([P, JH], F32, name="last_ps%d" % g, tag="bank%d" % (1 + g)) for g in range(2)]
+        for g in range(2):
+            second_product(first_ps[:, g, :], 0, g)
+        for g in range(2):
+            second_product(last_ps[g][:], 1, g)
+        p_sb = keep.tile([P, HALVES, 2, JH], F32, name="p_sb")
+        move(nc, True, p_sb[:, 0, :, :], first_ps[:])
+        for g in range(2):
+            move(nc, g == 0, page[g][:].indirect(page_list[:, 0:LH]), p_sb[:, 0, g, :])
+        for g in range(2):
+            move(nc, g == 0, p_sb[:, 1, g, :], last_ps[g][:])
+            move(nc, g == 0, page[g][:].indirect(page_list[:, LH : 2 * LH]), p_sb[:, 1, g, :])
         nc.scalar.dma_start(out=out[0:P, :], in_=page[0][:])
         nc.sync.dma_start(out=out[P : 2 * P, :], in_=page[1][:])

from contextlib import ExitStack

import concourse.mybir as mybir

K, T, J, R, C, N, E = 512, 1024, 256, 512, 512, 256, 1024
FLOPS = 2 * K * R * J * 2 + 2 * R * N * J

F32 = mybir.dt.float32
BF16 = mybir.dt.bfloat16
I32 = mybir.dt.int32
U32 = mybir.dt.uint32
U16 = mybir.dt.uint16
U8 = mybir.dt.uint8
E4M3 = mybir.dt.float8_e4m3fn_x4
E5M2 = mybir.dt.float8_e5m2_x4
E2M1 = mybir.dt.float4_e2m1fn_x4
COPY = mybir.ActivationFunctionType.Copy
ABS = mybir.ActivationFunctionType.Abs
SUB = mybir.AluOpType.subtract

P = 128
PACK = 4
HALVES = 2
JH = J // HALVES
LC = J // 16
LH = JH // 16


def load_scale_rows(queues, plane, scales):
    for q in range(4):
        queues[q].dma_start(out=plane[32 * q : 32 * q + 4, :].bitcast(I32), in_=scales[0, 4 * q : 4 * q + 4, :].bitcast(I32))


def move(nc, on_scalar, out, in_):
    if on_scalar:
        nc.scalar.activation(out=out, in_=in_, func=COPY)
    else:
        nc.vector.tensor_copy(out=out, in_=in_)


def tile_list_oneforboth_board_one_scattered_kernel(
    tc, xt_words, xt_scales, xo_words, xo_scales, w_words, w_scales, wb_words, wb_scales, offs, offs2, offs3, offs4, offs5, out
):
    nc = tc.nc
    with ExitStack() as ctx:
        lists = ctx.enter_context(tc.tile_pool(name="lists", bufs=1))
        keep = ctx.enter_context(tc.tile_pool(name="keep", bufs=1))
        psum = ctx.enter_context(tc.psum_pool(name="psum", bufs=1))

        token_list = lists.tile([P, LC], U16, name="token_list")
        note_list = lists.tile([P, LC], U16, name="note_list")
        put_list = lists.tile([P, LC], U16, name="put_list")
        read_list = lists.tile([P, LC], U16, name="read_list")
        page_list = lists.tile([P, LC], U16, name="page_list")

        xt_w = keep.tile([P, T], U32, name="xt_w", align_bytes=64)
        xt_s = keep.tile([P, T], U8, name="xt_s", align_bytes=64)
        xo_s = keep.tile([P, T], U8, name="xo_s", tag="page0", align_bytes=64)
        xo_w = keep.tile([P, T], U32, name="xo_w", align_bytes=64)
        w_raw = keep.tile([P, 2 * R], U8, name="w_raw", align_bytes=64)
        ws_raw = keep.tile([P, R], U8, name="ws_raw", tag="page1", align_bytes=64)
        wb_w = keep.tile([P, 2 * N], U8, name="wb_w", align_bytes=64)
        wb_s = keep.tile([P, N], U8, name="wb_s", align_bytes=64)
        board = [keep.tile([P, C], F32, name="board%d" % t, align_bytes=64) for t in range(PACK)]

        for plane in (xt_s, ws_raw, xo_s):
            nc.vector.memset(plane[:].bitcast(I32), 0)
        for t in (0, 1, 2, 3):
            nc.vector.memset(board[t][:], 0.0)
        nc.vector.memset(wb_s[:].bitcast(I32), 0)

        on_sync = [nc.sync] * 4
        nc.sync.dma_start(token_list[:], offs)
        load_scale_rows(on_sync, xt_s, xt_scales)
        nc.sync.dma_start(note_list[:], offs2)
        nc.sync.dma_start(out=w_raw[:].bitcast(I32), in_=w_words[0].bitcast(I32))
        nc.sync.dma_start(out=xt_w[:].bitcast(I32), in_=xt_words[0].rearrange("p c t -> p (c t)").bitcast(I32))
        load_scale_rows(on_sync, ws_raw, w_scales)
        nc.sync.dma_start(out=xo_w[:].bitcast(I32), in_=xo_words[0].rearrange("p c t -> p (c t)").bitcast(I32))
        load_scale_rows(on_sync, xo_s, xo_scales)
        nc.sync.dma_start(put_list[:], offs3)
        nc.sync.dma_start(read_list[:], offs4)
        nc.sync.dma_start(out=wb_w[:].bitcast(I32), in_=wb_words[0].bitcast(I32))
        load_scale_rows(on_sync, wb_s, wb_scales)
        nc.sync.dma_start(page_list[:], offs5)

        xtg_w = keep.tile([P, J], U32, name="xtg_w", align_bytes=64)
        xtg_s = keep.tile([P, J], U8, name="xtg_s", align_bytes=64)
        xog_w = keep.tile([P, J], U32, name="xog_w", align_bytes=64)
        xog_s = keep.tile([P, J], U8, name="xog_s", align_bytes=64)
        w_w = keep.tile([P, 2 * R], U8, name="w_w", align_bytes=64)
        w_s = keep.tile([P, R], U8, name="w_s", align_bytes=64)

        nc.vector.tensor_copy(out=xtg_s[:], in_=xt_s[:].indirect(token_list[:]))
        nc.vector.tensor_copy(
            out=w_w[:].bitcast(U16).rearrange("p (t m) -> p t m", t=PACK),
            in_=w_raw[:].bitcast(U16).rearrange("p (m t) -> p t m", t=PACK),
        )
        nc.vector.tensor_copy(out=xtg_w[:], in_=xt_w[:].indirect(token_list[:]))
        for t in (0, 1, 2, 3):
            nc.vector.tensor_copy(out=w_s[:, P * t : P * (t + 1)], in_=ws_raw[:, t : R : PACK])

        def first_product(acc, t, codes, scales):
            nc.tensor.matmul_mx(
                out=acc,
                lhsT=w_w[:, 2 * P * t : 2 * P * (t + 1)].bitcast(E2M1),
                lhsT_scale=w_s[:, P * t : P * (t + 1)],
                rhs=codes,
                rhs_scale=scales,
                start=True,
                stop=True,
            )

        a_ps = [psum.tile([P, J], F32, name="a_ps%d" % t, tag="bank%d" % t) for t in range(2)]
        a_ps23 = psum.tile([P, 2, J], F32, name="a_ps23", tag="bank2")
        for t in range(PACK):
            first_product(a_ps[t][:] if t < 2 else a_ps23[:, t - 2, :], t, xtg_w[:].bitcast(E5M2), xtg_s[:])

        nc.vector.tensor_copy(out=xog_w[:], in_=xo_w[:].indirect(note_list[:]))
        nc.vector.tensor_copy(out=xog_s[:], in_=xo_s[:].indirect(note_list[:]))
        b_ps = [psum.tile([P, PACK, JH], F32, name="b_ps%d" % h) for h in range(HALVES)]
        for h in range(HALVES):
            cols = slice(JH * h, JH * (h + 1))
            for t in range(PACK):
                first_product(b_ps[h][:, t, :], t, xog_w[:, cols].bitcast(E4M3), xog_s[:, cols])

        a_sb = [keep.tile([P, J], F32, name="a_sb%d" % t) for t in range(2)]
        a_sb23 = keep.tile([P, 2, J], F32, name="a_sb23", tag="page0", align_bytes=64)
        for t in range(2):
            move(nc, True, a_sb[t][:], a_ps[t][:])
        move(nc, False, a_sb23[:], a_ps23[:])
        for t in range(PACK):
            move(nc, t < 2, board[t][:].indirect(put_list[:]), a_sb[t][:] if t < 2 else a_sb23[:, t - 2, :])
        page = [keep.tile([P, E], F32, name="page%d" % g, tag="page%d" % g, align_bytes=64) for g in range(2)]
        for g in (1, 0):
            nc.gpsimd.memset(page[g][:], 0.0)

        picked = [keep.tile([P, PACK, JH], F32, name="picked%d" % h) for h in range(HALVES)]
        diff = [keep.tile([P, PACK, JH], F32, name="diff%d" % h) for h in range(HALVES)]
        hid = [keep.tile([P, JH, PACK], BF16, name="hid%d" % h, align_bytes=64) for h in range(HALVES)]
        hid_w = [keep.tile([P, JH], U32, name="hid_w%d" % h, align_bytes=64) for h in range(HALVES)]
        hid_s = [keep.tile([P, JH], U8, name="hid_s%d" % h, align_bytes=64) for h in range(HALVES)]
        for h in range(HALVES):
            for t in range(PACK):
                move(nc, (h, t) != (0, 3), picked[h][:, t, :], board[t][:].indirect(read_list[:, LH * h : LH * (h + 1)]))
        for h in range(HALVES):
            nc.vector.tensor_tensor(out=diff[h][:], in0=picked[h][:], in1=b_ps[h][:], op=SUB)
        for h in range(HALVES):
            nc.scalar.activation(
                out=hid[h][:].rearrange("p (c i) t -> p c t i", i=4),
                in_=diff[h][:].rearrange("p t (c i) -> p c t i", i=4),
                func=ABS,
            )
        for h in range(HALVES):
            nc.vector.quantize_mx(out=hid_w[h][:].bitcast(E4M3), scales=hid_s[h][:], in_=hid[h][:].rearrange("p j t -> p (j t)"))

        def second_product(acc, h, g):
            nc.tensor.matmul_mx(
                out=acc,
                lhsT=wb_w[:, 2 * P * g : 2 * P * (g + 1)].bitcast(E2M1),
                lhsT_scale=wb_s[:, P * g : P * (g + 1)],
                rhs=hid_w[h][:].bitcast(E4M3),
                rhs_scale=hid_s[h][:],
                start=True,
                stop=True,
            )

        first_ps = psum.tile([P, 2, JH], F32, name="first_ps", tag="bank0")
        last_ps = [psum.tile([P, JH], F32, name="last_ps%d" % g, tag="bank%d" % (1 + g)) for g in range(2)]
        for g in range(2):
            second_product(first_ps[:, g, :], 0, g)
        for g in range(2):
            second_product(last_ps[g][:], 1, g)
        p_sb = keep.tile([P, HALVES, 2, JH], F32, name="p_sb")
        move(nc, True, p_sb[:, 0, :, :], first_ps[:])
        for g in range(2):
            move(nc, g == 0, page[g][:].indirect(page_list[:, 0:LH]), p_sb[:, 0, g, :])
        for g in range(2):
            move(nc, g == 0, p_sb[:, 1, g, :], last_ps[g][:])
            move(nc, g == 0, page[g][:].indirect(page_list[:, LH : 2 * LH]), p_sb[:, 1, g, :])
        nc.scalar.dma_start(out=out[0:P, :], in_=page[0][:])
        nc.sync.dma_start(out=out[P : 2 * P, :], in_=page[1][:])
